import numpy as np
import ml_dtypes


def mxq(x, axis, fmt="e4m3"):
    dtype, down = {"e4m3": (ml_dtypes.float8_e4m3fn, 7), "e5m2": (ml_dtypes.float8_e5m2, 14)}[fmt]
    v = np.moveaxis(np.asarray(x, np.float32).astype(ml_dtypes.bfloat16).astype(np.float64), axis, -1)
    blocks = v.reshape(v.shape[:-1] + (-1, 32))
    amax = np.abs(blocks).max(-1, keepdims=True)
    byte = np.maximum(np.where(amax > 0, np.frexp(amax)[1] - 1 + 127, 0) - down, 1)
    scale = np.exp2(byte - 127.0)
    codes = (blocks / scale).astype(np.float32).astype(dtype).astype(np.float64)
    return np.moveaxis((codes * scale).reshape(v.shape), -1, axis)


WIDE = False


def mx_kscale(k):
    if not WIDE:
        return np.ones(k)
    levels = np.array([30, -30])
    if k % 512:
        return np.exp2(np.random.permutation(np.resize(levels, k // 32))).repeat(32)
    a = np.empty((k // 512, 16))
    for p in range(k // 512):
        a[p, :8] = np.random.permutation(np.resize(levels, 8))
        for g in range(8):
            far = levels[np.abs(levels - a[p, g]) >= 10]
            a[p, g + 8] = far[np.random.randint(len(far))]
    return np.exp2(a.ravel()).repeat(32)


def f64(x):
    return np.asarray(x).astype(np.float64)


def striped(idx):
    return np.tile(np.asarray(idx).reshape(-1, 16).T, (8, 1)).astype(np.uint16)


def unstriped(offs):
    return offs[:16].T.reshape(-1).astype(np.int64)


K, T, J, I, V, M = 1024, 1024, 256, 256, 1024, 128


def setup_inputs():
    n = np.random.standard_normal
    idx = np.random.permutation(T)[:J]
    idx2 = np.random.permutation(V)[:I]
    idx3 = np.random.permutation(I)[:M]
    fk = mx_kscale(K)
    return {
        "xf": (n((K, T)) * 0.03).astype(np.float32),
        "fk": (np.random.uniform(0.5, 2.0, (K, 1)) * fk[:, None]).astype(np.float32),
        "kf": (n((K, V))).astype(np.float32),
        "ko": (n((K, I)) * 0.6).astype(np.float32),
        "fi": (np.random.uniform(0.5, 2.0, (K, 1)) / fk[:, None]).astype(np.float32),
        "bi": (np.random.uniform(-0.7, 0.7, (1, I))).astype(np.float32),
        "rs": (1.0 * n((J, M))).astype(np.float32),
        "offs": striped(idx),
        "offs2": striped(idx2),
        "offs3": striped(idx3),
    }


def reference(xf, fk, kf, ko, fi, bi, rs, offs, offs2, offs3):
    idx = unstriped(offs)
    idx2 = unstriped(offs2)
    idx3 = unstriped(offs3)
    xg = f64(xf)[:, idx]
    x1 = np.pad(xg, ((0, 0), (1, 0)))[:, :J]
    u = (xg - 0.6 * x1) * f64(fk)
    vk = (f64(kf)[:, idx2] + f64(ko)) * f64(fi)
    uq = mxq(u, 0, "e5m2")
    vkq = mxq(vk, 0, "e5m2")
    a0 = uq.T @ vkq
    a = a0 + f64(bi)
    mn = np.mean(np.abs(a), axis=1, keepdims=True)
    y = a[:, idx3] / mn + 0.5 * f64(rs)
    return y

@@ -1,0 +1,189 @@
+from contextlib import ExitStack
+
+import concourse.mybir as mybir
+from concourse.masks import make_identity
+
+K, T, J, I, V, M = 1024, 1024, 256, 256, 1024, 128
+FLOPS = 2 * K * J * I
+
+F32 = mybir.dt.float32
+BF16 = mybir.dt.bfloat16
+U32 = mybir.dt.uint32
+U16 = mybir.dt.uint16
+U8 = mybir.dt.uint8
+E5M2X4 = mybir.dt.float8_e5m2_x4
+MULT = mybir.AluOpType.mult
+ADD = mybir.AluOpType.add
+COPY = mybir.ActivationFunctionType.Copy
+ABS = mybir.ActivationFunctionType.Abs
+
+P = 128
+PACK = 4
+K_PASS = P * PACK
+PASSES = K // K_PASS
+HALF = 128
+PAD = 8
+
+
+def tile_list_scores_steps_mixed_looked_f_kernel(tc, xf, fk, kf, ko, fi, bi, rs, offs, offs2, offs3, out):
+    nc = tc.nc
+    with ExitStack() as ctx:
+        lists = ctx.enter_context(tc.tile_pool(name="lists", bufs=1))
+        keep = ctx.enter_context(tc.tile_pool(name="keep", bufs=1))
+        psum = ctx.enter_context(tc.psum_pool(name="psum", bufs=1))
+
+        def rows(src, a):
+            return src[a * K_PASS : (a + 1) * K_PASS, :].rearrange("(p t) c -> p t c", t=PACK)
+
+        fk_t = keep.tile([P, PASSES, PACK], F32, name="fk_t")
+        fi_t = keep.tile([P, PASSES, PACK], F32, name="fi_t")
+        bi_t = keep.tile([P, 2], F32, name="bi_t")
+        nc.scalar.dma_start(out=fk_t[:], in_=fk.rearrange("(a p t) o -> p a (t o)", a=PASSES, t=PACK))
+        nc.scalar.dma_start(out=fi_t[:], in_=fi.rearrange("(a p t) o -> p a (t o)", a=PASSES, t=PACK))
+        nc.scalar.dma_start(out=bi_t[:], in_=bi.rearrange("o (p e) -> p (o e)", e=2))
+
+        list_x = lists.tile([P, J // 16], U16, name="list_x")
+        list_k = lists.tile([P, I // 16], U16, name="list_k")
+        list_a = lists.tile([P, M // 16], U16, name="list_a")
+
+        x0 = keep.tile([P, PACK, T], F32, name="x0")
+        k0 = keep.tile([P, PACK, V], F32, name="k0")
+        ko0 = keep.tile([P, PACK, I], F32, name="ko0")
+        x1 = [keep.tile([P, 2, T], F32, name="x1_%d" % h) for h in range(2)]
+        ko1 = keep.tile([P, PACK - 1, I], F32, name="ko1")
+        ko_last = keep.tile([P, I], F32, name="ko_last")
+        k1 = [keep.tile([P, V], F32, name="k1_%d" % t) for t in range(PACK)]
+        rs_t = keep.tile([P, 2, M], F32, name="rs_t")
+
+        nc.sync.dma_start(out=x0[:], in_=rows(xf, 0))
+        nc.sync.dma_start(list_x[:], offs)
+        nc.sync.dma_start(list_k[:], offs2)
+        nc.sync.dma_start(list_a[:], offs3)
+        nc.sync.dma_start(out=ko0[:], in_=rows(ko, 0))
+        nc.sync.dma_start(out=k0[:], in_=rows(kf, 0))
+        for h in range(2):
+            nc.sync.dma_start(out=x1[h][:], in_=rows(xf, 1)[:, 2 * h : 2 * h + 2, :])
+        nc.sync.dma_start(out=ko1[:], in_=rows(ko, 1)[:, 0 : PACK - 1, :])
+        for t in range(PACK - 1):
+            nc.sync.dma_start(out=k1[t][:], in_=rows(kf, 1)[:, t, :])
+        nc.sync.dma_start(out=ko_last[:], in_=rows(ko, 1)[:, PACK - 1, :])
+        nc.sync.dma_start(out=k1[PACK - 1][:], in_=rows(kf, 1)[:, PACK - 1, :])
+        nc.sync.dma_start(out=rs_t[:], in_=rs.rearrange("(m p) c -> p m c", p=P))
+
+        ident = keep.tile([P, P], F32, name="ident")
+        make_identity(nc, ident[:])
+        bias_ps = psum.tile([P, 2, P], F32, name="bias_ps")
+        for e in range(2):
+            nc.tensor.transpose(bias_ps[:, e, :], bi_t[:, e : e + 1].to_broadcast([P, P]), ident[:])
+        bias = keep.tile([P, I], F32, name="bias")
+        nc.vector.tensor_copy(
+            out=bias[:].rearrange("p (n e) -> p n e", e=2), in_=bias_ps[:].rearrange("p e n -> p n e")
+        )
+
+        xg = keep.tile([P, PASSES * PACK, PAD + J], F32, name="xg")
+        nc.vector.memset(xg[:, :, PAD - 1 : PAD], 0.0)
+
+        u_codes = [keep.tile([P, J], U32, name="u_codes%d" % a, align_bytes=64) for a in range(PASSES)]
+        u_scales = [keep.tile([P, J], U8, name="u_scales%d" % a, align_bytes=64) for a in range(PASSES)]
+
+        def quantise(codes, scales, woven):
+            nc.vector.quantize_mx(
+                out=codes.bitcast(E5M2X4), scales=scales, in_=woven[:].rearrange("p c t -> p (c t)")
+            )
+
+        def token_pass(a, windows):
+            woven = keep.tile([P, J, PACK], BF16, name="u_woven%d" % a, align_bytes=64)
+            diffs = []
+            for t in range(PACK + 1):
+                if t < PACK:
+                    s = a * PACK + t
+                    nc.scalar.activation(xg[:, s, PAD:], windows[t].indirect(list_x[:]), COPY)
+                    diff = keep.tile([P, J], F32, name="diff%d" % s)
+                    nc.vector.scalar_tensor_tensor(
+                        diff[:], xg[:, s, PAD - 1 : PAD - 1 + J], -0.6, xg[:, s, PAD:], MULT, ADD
+                    )
+                    diffs.append(diff)
+                if t > 0:
+                    nc.vector.tensor_scalar(
+                        woven[:, :, t - 1], diffs[t - 1][:], fk_t[:, a, t - 1 : t], None, MULT
+                    )
+            quantise(u_codes[a][:], u_scales[a][:], woven)
+
+        acc = [psum.tile([P, I], F32, name="acc%d" % m) for m in range(2)]
+
+        def product(m, a, cols, codes, scales, start, stop):
+            js = slice(m * P, (m + 1) * P)
+            nc.tensor.matmul_mx(
+                out=acc[m][:, cols],
+                lhsT=u_codes[a][:, js].bitcast(E5M2X4),
+                lhsT_scale=u_scales[a][:, js],
+                rhs=codes.bitcast(E5M2X4),
+                rhs_scale=scales,
+                start=start,
+                stop=stop,
+            )
+
+        token_pass(0, [x0[:, t, :] for t in range(PACK)])
+        woven0 = keep.tile([P, I, PACK], BF16, name="v_woven0", align_bytes=64)
+        sums = []
+        for t in range(PACK + 1):
+            if t < PACK:
+                kg = keep.tile([P, I], F32, name="kg0_%d" % t)
+                nc.scalar.activation(kg[:], k0[:, t, :].indirect(list_k[:]), COPY)
+                ks = keep.tile([P, I], F32, name="ks0_%d" % t)
+                nc.vector.tensor_tensor(ks[:], kg[:], ko0[:, t, :], ADD)
+                sums.append(ks)
+            if t > 0:
+                nc.vector.tensor_scalar(woven0[:, :, t - 1], sums[t - 1][:], fi_t[:, 0, t - 1 : t], None, MULT)
+        v_codes0 = keep.tile([P, I], U32, name="v_codes0", align_bytes=64)
+        v_scales0 = keep.tile([P, I], U8, name="v_scales0", align_bytes=64)
+        quantise(v_codes0[:], v_scales0[:], woven0)
+        for m in range(2):
+            product(m, 0, slice(0, I), v_codes0[:], v_scales0[:], True, False)
+
+        token_pass(1, [x1[t // 2][:, t % 2, :] for t in range(PACK)])
+        woven1 = [keep.tile([P, HALF, PACK], BF16, name="v_woven1_%d" % h, align_bytes=64) for h in range(2)]
+        for t in range(PACK):
+            own = ko1[:, t, :] if t < PACK - 1 else ko_last[:]
+            ks = [keep.tile([P, HALF], F32, name="ks1_%d_%d" % (t, h)) for h in range(2)]
+            if t < 2:
+                kg = keep.tile([P, I], F32, name="kg1_%d" % t)
+                nc.scalar.activation(kg[:], k1[t][:].indirect(list_k[:]), COPY)
+            for h in range(2):
+                cols = slice(h * HALF, (h + 1) * HALF)
+                if t < 2:
+                    nc.vector.tensor_tensor(ks[h][:], kg[:, cols], own[:, cols], ADD)
+                else:
+                    piece = list_k[:, h * HALF // 16 : (h + 1) * HALF // 16]
+                    nc.vector.tensor_tensor(ks[h][:], k1[t][:].indirect(piece), own[:, cols], ADD)
+            for h in range(2):
+                nc.vector.tensor_scalar(woven1[h][:, :, t], ks[h][:], fi_t[:, 1, t : t + 1], None, MULT)
+        for h in range(2):
+            codes = keep.tile([P, HALF], U32, name="v_codes1_%d" % h, align_bytes=64)
+            scales = keep.tile([P, HALF], U8, name="v_scales1_%d" % h, align_bytes=64)
+            quantise(codes[:], scales[:], woven1[h])
+            for m in range(2):
+                product(m, 1, slice(h * HALF, (h + 1) * HALF), codes[:], scales[:], False, h == 1)
+
+        half_rs = keep.tile([P, 2, M], F32, name="half_rs")
+        nc.scalar.activation(half_rs[:], rs_t[:], COPY, scale=0.5)
+
+        scores, means, picked = [], [], []
+        for m in range(2):
+            sc = keep.tile([P, I], F32, name="scores%d" % m)
+            nc.vector.tensor_tensor(sc[:], acc[m][:], bias[:], ADD)
+            scores.append(sc)
+        for m in range(2):
+            mag = keep.tile([P, I], F32, name="mag%d" % m)
+            mean = keep.tile([P, 1], F32, name="mean%d" % m)
+            nc.scalar.activation(mag[:], scores[m][:], ABS, scale=1.0 / I, accum_out=mean[:])
+            means.append(mean)
+            pk = keep.tile([P, M], F32, name="picked%d" % m)
+            nc.vector.tensor_copy(pk[:], scores[m][:].indirect(list_a[:]))
+            picked.append(pk)
+        for m in range(2):
+            inv = keep.tile([P, 1], F32, name="inv%d" % m)
+            nc.vector.reciprocal(inv[:], means[m][:])
+            y = keep.tile([P, M], F32, name="y%d" % m)
+            nc.vector.scalar_tensor_tensor(y[:], picked[m][:], inv[:], half_rs[:, m, :], MULT, ADD)
+            nc.sync.dma_start(out=out[m * P : (m + 1) * P, :], in_=y[:])

@@ -38,46 +38,52 @@ def tile_list_scores_steps_mixed_looked_f_kernel(tc, xf, fk, kf, ko, fi, bi, rs,
         fk_t = keep.tile([P, PASSES, PACK], F32, name="fk_t")
         fi_t = keep.tile([P, PASSES, PACK], F32, name="fi_t")
         bi_t = keep.tile([P, 2], F32, name="bi_t")
-        nc.scalar.dma_start(out=fk_t[:], in_=fk.rearrange("(a p t) o -> p a (t o)", a=PASSES, t=PACK))
-        nc.scalar.dma_start(out=fi_t[:], in_=fi.rearrange("(a p t) o -> p a (t o)", a=PASSES, t=PACK))
-        nc.scalar.dma_start(out=bi_t[:], in_=bi.rearrange("o (p e) -> p (o e)", e=2))
+        nc.sync.dma_start(out=bi_t[:], in_=bi.rearrange("o (p e) -> p (o e)", e=2))
 
         list_x = lists.tile([P, J // 16], U16, name="list_x")
         list_k = lists.tile([P, I // 16], U16, name="list_k")
         list_a = lists.tile([P, M // 16], U16, name="list_a")
 
-        x0 = keep.tile([P, PACK, T], F32, name="x0")
-        k0 = keep.tile([P, PACK, V], F32, name="k0")
+        x0 = [keep.tile([P, 2, T], F32, name="x0_%d" % h) for h in range(2)]
+        k0 = [keep.tile([P, 2, V], F32, name="k0_%d" % h) for h in range(2)]
         ko0 = keep.tile([P, PACK, I], F32, name="ko0")
-        x1 = [keep.tile([P, 2, T], F32, name="x1_%d" % h) for h in range(2)]
+        x1_pair = keep.tile([P, 2, T], F32, name="x1_pair")
+        x1 = [keep.tile([P, T], F32, name="x1_%d" % t) for t in (2, 3)]
         ko1 = keep.tile([P, PACK - 1, I], F32, name="ko1")
         ko_last = keep.tile([P, I], F32, name="ko_last")
         k1 = [keep.tile([P, V], F32, name="k1_%d" % t) for t in range(PACK)]
         rs_t = keep.tile([P, 2, M], F32, name="rs_t")
 
-        nc.sync.dma_start(out=x0[:], in_=rows(xf, 0))
+        nc.sync.dma_start(out=x0[0][:], in_=rows(xf, 0)[:, 0:2, :])
         nc.sync.dma_start(list_x[:], offs)
+        nc.sync.dma_start(out=fk_t[:], in_=fk.rearrange("(a p t) o -> p a (t o)", a=PASSES, t=PACK))
+        nc.sync.dma_start(out=x0[1][:], in_=rows(xf, 0)[:, 2:4, :])
         nc.sync.dma_start(list_k[:], offs2)
-        nc.sync.dma_start(list_a[:], offs3)
+        nc.sync.dma_start(out=fi_t[:], in_=fi.rearrange("(a p t) o -> p a (t o)", a=PASSES, t=PACK))
         nc.sync.dma_start(out=ko0[:], in_=rows(ko, 0))
-        nc.sync.dma_start(out=k0[:], in_=rows(kf, 0))
         for h in range(2):
-            nc.sync.dma_start(out=x1[h][:], in_=rows(xf, 1)[:, 2 * h : 2 * h + 2, :])
+            nc.sync.dma_start(out=k0[h][:], in_=rows(kf, 0)[:, 2 * h : 2 * h + 2, :])
+        nc.sync.dma_start(out=x1_pair[:], in_=rows(xf, 1)[:, 0:2, :])
+        for t in (2, 3):
+            nc.sync.dma_start(out=x1[t - 2][:], in_=rows(xf, 1)[:, t, :])
         nc.sync.dma_start(out=ko1[:], in_=rows(ko, 1)[:, 0 : PACK - 1, :])
         for t in range(PACK - 1):
             nc.sync.dma_start(out=k1[t][:], in_=rows(kf, 1)[:, t, :])
         nc.sync.dma_start(out=ko_last[:], in_=rows(ko, 1)[:, PACK - 1, :])
         nc.sync.dma_start(out=k1[PACK - 1][:], in_=rows(kf, 1)[:, PACK - 1, :])
+        nc.sync.dma_start(list_a[:], offs3)
         nc.sync.dma_start(out=rs_t[:], in_=rs.rearrange("(m p) c -> p m c", p=P))
 
         ident = keep.tile([P, P], F32, name="ident")
         make_identity(nc, ident[:])
         bias_ps = psum.tile([P, 2, P], F32, name="bias_ps")
+        bi_wide = keep.tile([P, 2, P], F32, name="bi_wide")
+        nc.scalar.activation(bi_wide[:], bi_t[:].unsqueeze(2).to_broadcast([P, 2, P]), COPY)
         for e in range(2):
-            nc.tensor.transpose(bias_ps[:, e, :], bi_t[:, e : e + 1].to_broadcast([P, P]), ident[:])
+            nc.tensor.transpose(bias_ps[:, e, :], bi_wide[:, e, :], ident[:])
         bias = keep.tile([P, I], F32, name="bias")
-        nc.vector.tensor_copy(
-            out=bias[:].rearrange("p (n e) -> p n e", e=2), in_=bias_ps[:].rearrange("p e n -> p n e")
+        nc.scalar.activation(
+            bias[:].rearrange("p (n e) -> p n e", e=2), bias_ps[:].rearrange("p e n -> p n e"), COPY
         )
 
         xg = keep.tile([P, PASSES * PACK, PAD + J], F32, name="xg")
@@ -109,27 +115,28 @@ def tile_list_scores_steps_mixed_looked_f_kernel(tc, xf, fk, kf, ko, fi, bi, rs,
                     )
             quantise(u_codes[a][:], u_scales[a][:], woven)
 
-        acc = [psum.tile([P, I], F32, name="acc%d" % m) for m in range(2)]
+        acc = [[psum.tile([P, HALF], F32, name="acc%d_%d" % (m, h)) for h in range(2)] for m in range(2)]
+        halves = [slice(0, HALF), slice(HALF, I)]
 
-        def product(m, a, cols, codes, scales, start, stop):
+        def product(m, a, h, codes, scales):
             js = slice(m * P, (m + 1) * P)
             nc.tensor.matmul_mx(
-                out=acc[m][:, cols],
+                out=acc[m][h][:],
                 lhsT=u_codes[a][:, js].bitcast(E5M2X4),
                 lhsT_scale=u_scales[a][:, js],
                 rhs=codes.bitcast(E5M2X4),
                 rhs_scale=scales,
-                start=start,
-                stop=stop,
+                start=(a == 0),
+                stop=(a == PASSES - 1),
             )
 
-        token_pass(0, [x0[:, t, :] for t in range(PACK)])
+        token_pass(0, [x0[t // 2][:, t % 2, :] for t in range(PACK)])
         woven0 = keep.tile([P, I, PACK], BF16, name="v_woven0", align_bytes=64)
         sums = []
         for t in range(PACK + 1):
             if t < PACK:
                 kg = keep.tile([P, I], F32, name="kg0_%d" % t)
-                nc.scalar.activation(kg[:], k0[:, t, :].indirect(list_k[:]), COPY)
+                nc.scalar.activation(kg[:], k0[t // 2][:, t % 2, :].indirect(list_k[:]), COPY)
                 ks = keep.tile([P, I], F32, name="ks0_%d" % t)
                 nc.vector.tensor_tensor(ks[:], kg[:], ko0[:, t, :], ADD)
                 sums.append(ks)
@@ -139,51 +146,56 @@ def tile_list_scores_steps_mixed_looked_f_kernel(tc, xf, fk, kf, ko, fi, bi, rs,
         v_scales0 = keep.tile([P, I], U8, name="v_scales0", align_bytes=64)
         quantise(v_codes0[:], v_scales0[:], woven0)
         for m in range(2):
-            product(m, 0, slice(0, I), v_codes0[:], v_scales0[:], True, False)
+            for h in range(2):
+                product(m, 0, h, v_codes0[:, halves[h]], v_scales0[:, halves[h]])
 
-        token_pass(1, [x1[t // 2][:, t % 2, :] for t in range(PACK)])
+        token_pass(1, [x1_pair[:, 0, :], x1_pair[:, 1, :], x1[0][:], x1[1][:]])
         woven1 = [keep.tile([P, HALF, PACK], BF16, name="v_woven1_%d" % h, align_bytes=64) for h in range(2)]
         for t in range(PACK):
             own = ko1[:, t, :] if t < PACK - 1 else ko_last[:]
-            ks = [keep.tile([P, HALF], F32, name="ks1_%d_%d" % (t, h)) for h in range(2)]
-            if t < 2:
-                kg = keep.tile([P, I], F32, name="kg1_%d" % t)
-                nc.scalar.activation(kg[:], k1[t][:].indirect(list_k[:]), COPY)
+            ks = []
             for h in range(2):
-                cols = slice(h * HALF, (h + 1) * HALF)
-                if t < 2:
-                    nc.vector.tensor_tensor(ks[h][:], kg[:, cols], own[:, cols], ADD)
+                listed = k1[t][:].indirect(list_k[:, h * HALF // 16 : (h + 1) * HALF // 16])
+                total = keep.tile([P, HALF], F32, name="ks1_%d_%d" % (t, h), tag="ks1_%d_%d" % (min(t, 2) if h == 0 else t, h))
+                if t == PACK - 1 and h == 0:
+                    nc.vector.tensor_tensor(total[:], listed, own[:, halves[h]], ADD)
                 else:
-                    piece = list_k[:, h * HALF // 16 : (h + 1) * HALF // 16]
-                    nc.vector.tensor_tensor(ks[h][:], k1[t][:].indirect(piece), own[:, cols], ADD)
+                    kg = keep.tile([P, HALF], F32, name="kg1_%d_%d" % (t, h))
+                    nc.scalar.activation(kg[:], listed, COPY)
+                    nc.vector.tensor_tensor(total[:], kg[:], own[:, halves[h]], ADD)
+                ks.append(total[:])
             for h in range(2):
-                nc.vector.tensor_scalar(woven1[h][:, :, t], ks[h][:], fi_t[:, 1, t : t + 1], None, MULT)
+                nc.vector.tensor_scalar(woven1[h][:, :, t], ks[h], fi_t[:, 1, t : t + 1], None, MULT)
         for h in range(2):
             codes = keep.tile([P, HALF], U32, name="v_codes1_%d" % h, align_bytes=64)
             scales = keep.tile([P, HALF], U8, name="v_scales1_%d" % h, align_bytes=64)
             quantise(codes[:], scales[:], woven1[h])
             for m in range(2):
-                product(m, 1, slice(h * HALF, (h + 1) * HALF), codes[:], scales[:], False, h == 1)
+                product(m, 1, h, codes[:], scales[:])
 
         half_rs = keep.tile([P, 2, M], F32, name="half_rs")
         nc.scalar.activation(half_rs[:], rs_t[:], COPY, scale=0.5)
 
-        scores, means, picked = [], [], []
+        scores = [keep.tile([P, I + PAD], F32, name="scores%d" % m) for m in range(2)]
+        means = [keep.tile([P, 1], F32, name="mean%d" % m) for m in range(2)]
+        for h in range(2):
+            for m in range(2):
+                nc.vector.tensor_tensor(scores[m][:, halves[h]], acc[m][h][:], bias[:, halves[h]], ADD)
+            for m in range(2):
+                mag = keep.tile([P, HALF + 1], F32, name="mag%d_%d" % (m, h))
+                if h == 0:
+                    nc.scalar.activation(mag[:, :HALF], scores[m][:, :HALF], ABS, accum_out=scores[m][:, I : I + 1])
+                else:
+                    nc.scalar.activation(
+                        mag[:], scores[m][:, HALF : I + 1], ABS, scale=1.0 / I, accum_out=means[m][:]
+                    )
+        picked = [keep.tile([P, M], F32, name="picked%d" % m) for m in range(2)]
+        nc.vector.tensor_copy(picked[0][:], scores[0][:, :I].indirect(list_a[:]))
+        nc.scalar.activation(picked[1][:], scores[1][:, :I].indirect(list_a[:]), COPY)
+        invs = [keep.tile([P, 1], F32, name="inv%d" % m) for m in range(2)]
         for m in range(2):
-            sc = keep.tile([P, I], F32, name="scores%d" % m)
-            nc.vector.tensor_tensor(sc[:], acc[m][:], bias[:], ADD)
-            scores.append(sc)
+            nc.vector.reciprocal(invs[m][:], means[m][:])
         for m in range(2):
-            mag = keep.tile([P, I], F32, name="mag%d" % m)
-            mean = keep.tile([P, 1], F32, name="mean%d" % m)
-            nc.scalar.activation(mag[:], scores[m][:], ABS, scale=1.0 / I, accum_out=mean[:])
-            means.append(mean)
-            pk = keep.tile([P, M], F32, name="picked%d" % m)
-            nc.vector.tensor_copy(pk[:], scores[m][:].indirect(list_a[:]))
-            picked.append(pk)
-        for m in range(2):
-            inv = keep.tile([P, 1], F32, name="inv%d" % m)
-            nc.vector.reciprocal(inv[:], means[m][:])
             y = keep.tile([P, M], F32, name="y%d" % m)
-            nc.vector.scalar_tensor_tensor(y[:], picked[m][:], inv[:], half_rs[:, m, :], MULT, ADD)
+            nc.vector.scalar_tensor_tensor(y[:], picked[m][:], invs[m][:], half_rs[:, m, :], MULT, ADD)
             nc.sync.dma_start(out=out[m * P : (m + 1) * P, :], in_=y[:])

@@ -23,6 +23,7 @@ K_PASS = P * PACK
 PASSES = K // K_PASS
 HALF = 128
 PAD = 8
+BIAS_ROW = 32
 
 
 def tile_list_scores_steps_mixed_looked_f_kernel(tc, xf, fk, kf, ko, fi, bi, rs, offs, offs2, offs3, out):
@@ -35,37 +36,32 @@ def tile_list_scores_steps_mixed_looked_f_kernel(tc, xf, fk, kf, ko, fi, bi, rs,
         def rows(src, a):
             return src[a * K_PASS : (a + 1) * K_PASS, :].rearrange("(p t) c -> p t c", t=PACK)
 
-        fk_t = keep.tile([P, PASSES, PACK], F32, name="fk_t")
-        fi_t = keep.tile([P, PASSES, PACK], F32, name="fi_t")
-        bi_t = keep.tile([P, 2], F32, name="bi_t")
-        nc.sync.dma_start(out=bi_t[:], in_=bi.rearrange("o (p e) -> p (o e)", e=2))
+        vectors = keep.tile([P, K_PASS], F32, name="vectors", tag="vectors_then_xg")
 
         list_x = lists.tile([P, J // 16], U16, name="list_x")
         list_k = lists.tile([P, I // 16], U16, name="list_k")
         list_a = lists.tile([P, M // 16], U16, name="list_a")
 
-        x0 = [keep.tile([P, 2, T], F32, name="x0_%d" % h) for h in range(2)]
+        x0 = keep.tile([P, PACK, T], F32, name="x0")
         k0 = [keep.tile([P, 2, V], F32, name="k0_%d" % h) for h in range(2)]
         ko0 = keep.tile([P, PACK, I], F32, name="ko0")
-        x1_pair = keep.tile([P, 2, T], F32, name="x1_pair")
-        x1 = [keep.tile([P, T], F32, name="x1_%d" % t) for t in (2, 3)]
+        x1 = [keep.tile([P, 2, T], F32, name="x1_%d" % h) for h in range(2)]
         ko1 = keep.tile([P, PACK - 1, I], F32, name="ko1")
         ko_last = keep.tile([P, I], F32, name="ko_last")
         k1 = [keep.tile([P, V], F32, name="k1_%d" % t) for t in range(PACK)]
         rs_t = keep.tile([P, 2, M], F32, name="rs_t")
 
-        nc.sync.dma_start(out=x0[0][:], in_=rows(xf, 0)[:, 0:2, :])
+        nc.sync.dma_start(out=x0[:], in_=rows(xf, 0))
         nc.sync.dma_start(list_x[:], offs)
-        nc.sync.dma_start(out=fk_t[:], in_=fk.rearrange("(a p t) o -> p a (t o)", a=PASSES, t=PACK))
-        nc.sync.dma_start(out=x0[1][:], in_=rows(xf, 0)[:, 2:4, :])
+        nc.sync.dma_start(out=vectors[BIAS_ROW : BIAS_ROW + 1, :I], in_=bi)
+        nc.sync.dma_start(out=vectors[:PASSES, :], in_=fk.rearrange("(a c) o -> a (c o)", a=PASSES))
+        nc.sync.dma_start(out=vectors[PASSES : 2 * PASSES, :], in_=fi.rearrange("(a c) o -> a (c o)", a=PASSES))
         nc.sync.dma_start(list_k[:], offs2)
-        nc.sync.dma_start(out=fi_t[:], in_=fi.rearrange("(a p t) o -> p a (t o)", a=PASSES, t=PACK))
         nc.sync.dma_start(out=ko0[:], in_=rows(ko, 0))
         for h in range(2):
             nc.sync.dma_start(out=k0[h][:], in_=rows(kf, 0)[:, 2 * h : 2 * h + 2, :])
-        nc.sync.dma_start(out=x1_pair[:], in_=rows(xf, 1)[:, 0:2, :])
-        for t in (2, 3):
-            nc.sync.dma_start(out=x1[t - 2][:], in_=rows(xf, 1)[:, t, :])
+        for h in range(2):
+            nc.sync.dma_start(out=x1[h][:], in_=rows(xf, 1)[:, 2 * h : 2 * h + 2, :])
         nc.sync.dma_start(out=ko1[:], in_=rows(ko, 1)[:, 0 : PACK - 1, :])
         for t in range(PACK - 1):
             nc.sync.dma_start(out=k1[t][:], in_=rows(kf, 1)[:, t, :])
@@ -76,17 +72,34 @@ def tile_list_scores_steps_mixed_looked_f_kernel(tc, xf, fk, kf, ko, fi, bi, rs,
 
         ident = keep.tile([P, P], F32, name="ident")
         make_identity(nc, ident[:])
-        bias_ps = psum.tile([P, 2, P], F32, name="bias_ps")
-        bi_wide = keep.tile([P, 2, P], F32, name="bi_wide")
-        nc.scalar.activation(bi_wide[:], bi_t[:].unsqueeze(2).to_broadcast([P, 2, P]), COPY)
-        for e in range(2):
-            nc.tensor.transpose(bias_ps[:, e, :], bi_wide[:, e, :], ident[:])
+        dealt = keep.tile([P, PACK, P], F32, name="dealt")
+        nc.scalar.activation(dealt[:], ident[:].unsqueeze(1).to_broadcast([P, PACK, P]), COPY, scale=0.0)
+        nc.vector.tensor_copy(
+            dealt[: 2 * PASSES, :, :], vectors[: 2 * PASSES, :].rearrange("r (p t) -> r t p", t=PACK)
+        )
+        nc.scalar.activation(
+            dealt[BIAS_ROW : BIAS_ROW + 1, :, : I // PACK],
+            vectors[BIAS_ROW : BIAS_ROW + 1, :I].rearrange("r (p t) -> r t p", t=PACK),
+            COPY,
+        )
+        turned = psum.tile([P, PACK, P], F32, name="turned")
+        for t in range(PACK):
+            nc.tensor.transpose(turned[:, t, :], dealt[:, t, :], ident[:])
+        factors = keep.tile([P, PACK, 2 * PASSES], F32, name="factors")
+        nc.vector.tensor_copy(factors[:], turned[:, :, : 2 * PASSES])
+        bias_cols = keep.tile([P, PACK], F32, name="bias_cols")
+        nc.vector.tensor_copy(bias_cols[:], turned[:, :, BIAS_ROW])
+        bias_ps = psum.tile([P, PACK, P], F32, name="bias_ps")
+        for t in range(PACK):
+            nc.tensor.transpose(bias_ps[:, t, :], bias_cols[:, t : t + 1].to_broadcast([P, P]), ident[:])
         bias = keep.tile([P, I], F32, name="bias")
         nc.scalar.activation(
-            bias[:].rearrange("p (n e) -> p n e", e=2), bias_ps[:].rearrange("p e n -> p n e"), COPY
+            bias[:].rearrange("p (n t) -> p n t", t=PACK),
+            bias_ps[:, :, : I // PACK].rearrange("p t n -> p n t"),
+            COPY,
         )
 
-        xg = keep.tile([P, PASSES * PACK, PAD + J], F32, name="xg")
+        xg = keep.tile([P, PASSES * PACK, PAD + J], F32, name="xg", tag="vectors_then_xg")
         nc.vector.memset(xg[:, :, PAD - 1 : PAD], 0.0)
 
         u_codes = [keep.tile([P, J], U32, name="u_codes%d" % a, align_bytes=64) for a in range(PASSES)]
@@ -111,7 +124,7 @@ def tile_list_scores_steps_mixed_looked_f_kernel(tc, xf, fk, kf, ko, fi, bi, rs,
                     diffs.append(diff)
                 if t > 0:
                     nc.vector.tensor_scalar(
-                        woven[:, :, t - 1], diffs[t - 1][:], fk_t[:, a, t - 1 : t], None, MULT
+                        woven[:, :, t - 1], diffs[t - 1][:], factors[:, t - 1, a : a + 1], None, MULT
                     )
             quantise(u_codes[a][:], u_scales[a][:], woven)
 
@@ -130,7 +143,7 @@ def tile_list_scores_steps_mixed_looked_f_kernel(tc, xf, fk, kf, ko, fi, bi, rs,
                 stop=(a == PASSES - 1),
             )
 
-        token_pass(0, [x0[t // 2][:, t % 2, :] for t in range(PACK)])
+        token_pass(0, [x0[:, t, :] for t in range(PACK)])
         woven0 = keep.tile([P, I, PACK], BF16, name="v_woven0", align_bytes=64)
         sums = []
         for t in range(PACK + 1):
@@ -141,7 +154,7 @@ def tile_list_scores_steps_mixed_looked_f_kernel(tc, xf, fk, kf, ko, fi, bi, rs,
                 nc.vector.tensor_tensor(ks[:], kg[:], ko0[:, t, :], ADD)
                 sums.append(ks)
             if t > 0:
-                nc.vector.tensor_scalar(woven0[:, :, t - 1], sums[t - 1][:], fi_t[:, 0, t - 1 : t], None, MULT)
+                nc.vector.tensor_scalar(woven0[:, :, t - 1], sums[t - 1][:], factors[:, t - 1, PASSES : PASSES + 1], None, MULT)
         v_codes0 = keep.tile([P, I], U32, name="v_codes0", align_bytes=64)
         v_scales0 = keep.tile([P, I], U8, name="v_scales0", align_bytes=64)
         quantise(v_codes0[:], v_scales0[:], woven0)
@@ -149,7 +162,7 @@ def tile_list_scores_steps_mixed_looked_f_kernel(tc, xf, fk, kf, ko, fi, bi, rs,
             for h in range(2):
                 product(m, 0, h, v_codes0[:, halves[h]], v_scales0[:, halves[h]])
 
-        token_pass(1, [x1_pair[:, 0, :], x1_pair[:, 1, :], x1[0][:], x1[1][:]])
+        token_pass(1, [x1[t // 2][:, t % 2, :] for t in range(PACK)])
         woven1 = [keep.tile([P, HALF, PACK], BF16, name="v_woven1_%d" % h, align_bytes=64) for h in range(2)]
         for t in range(PACK):
             own = ko1[:, t, :] if t < PACK - 1 else ko_last[:]
@@ -165,7 +178,7 @@ def tile_list_scores_steps_mixed_looked_f_kernel(tc, xf, fk, kf, ko, fi, bi, rs,
                     nc.vector.tensor_tensor(total[:], kg[:], own[:, halves[h]], ADD)
                 ks.append(total[:])
             for h in range(2):
-                nc.vector.tensor_scalar(woven1[h][:, :, t], ks[h], fi_t[:, 1, t : t + 1], None, MULT)
+                nc.vector.tensor_scalar(woven1[h][:, :, t], ks[h], factors[:, t, PASSES + 1 : PASSES + 2], None, MULT)
         for h in range(2):
             codes = keep.tile([P, HALF], U32, name="v_codes1_%d" % h, align_bytes=64)
             scales = keep.tile([P, HALF], U8, name="v_scales1_%d" % h, align_bytes=64)

from contextlib import ExitStack

import concourse.mybir as mybir
from concourse.masks import make_identity

K, T, J, I, V, M = 1024, 1024, 256, 256, 1024, 128
FLOPS = 2 * K * J * I

F32 = mybir.dt.float32
BF16 = mybir.dt.bfloat16
U32 = mybir.dt.uint32
U16 = mybir.dt.uint16
U8 = mybir.dt.uint8
E5M2X4 = mybir.dt.float8_e5m2_x4
MULT = mybir.AluOpType.mult
ADD = mybir.AluOpType.add
COPY = mybir.ActivationFunctionType.Copy
ABS = mybir.ActivationFunctionType.Abs

P = 128
PACK = 4
K_PASS = P * PACK
PASSES = K // K_PASS
HALF = 128
PAD = 8
BIAS_ROW = 32


def tile_list_scores_steps_mixed_looked_f_kernel(tc, xf, fk, kf, ko, fi, bi, rs, offs, offs2, offs3, out):
    nc = tc.nc
    with ExitStack() as ctx:
        lists = ctx.enter_context(tc.tile_pool(name="lists", bufs=1))
        keep = ctx.enter_context(tc.tile_pool(name="keep", bufs=1))
        psum = ctx.enter_context(tc.psum_pool(name="psum", bufs=1))

        def rows(src, a):
            return src[a * K_PASS : (a + 1) * K_PASS, :].rearrange("(p t) c -> p t c", t=PACK)

        vectors = keep.tile([P, K_PASS], F32, name="vectors", tag="vectors_then_xg")

        list_x = lists.tile([P, J // 16], U16, name="list_x")
        list_k = lists.tile([P, I // 16], U16, name="list_k")
        list_a = lists.tile([P, M // 16], U16, name="list_a")

        x0 = keep.tile([P, PACK, T], F32, name="x0")
        k0 = [keep.tile([P, 2, V], F32, name="k0_%d" % h) for h in range(2)]
        ko0 = keep.tile([P, PACK, I], F32, name="ko0")
        x1 = [keep.tile([P, 2, T], F32, name="x1_%d" % h) for h in range(2)]
        ko1 = keep.tile([P, PACK - 1, I], F32, name="ko1")
        ko_last = keep.tile([P, I], F32, name="ko_last")
        k1 = [keep.tile([P, V], F32, name="k1_%d" % t) for t in range(PACK)]
        rs_t = keep.tile([P, 2, M], F32, name="rs_t")

        nc.sync.dma_start(out=x0[:], in_=rows(xf, 0))
        nc.sync.dma_start(list_x[:], offs)
        nc.sync.dma_start(out=vectors[BIAS_ROW : BIAS_ROW + 1, :I], in_=bi)
        nc.sync.dma_start(out=vectors[:PASSES, :], in_=fk.rearrange("(a c) o -> a (c o)", a=PASSES))
        nc.sync.dma_start(out=vectors[PASSES : 2 * PASSES, :], in_=fi.rearrange("(a c) o -> a (c o)", a=PASSES))
        nc.sync.dma_start(list_k[:], offs2)
        nc.sync.dma_start(out=ko0[:], in_=rows(ko, 0))
        for h in range(2):
            nc.sync.dma_start(out=k0[h][:], in_=rows(kf, 0)[:, 2 * h : 2 * h + 2, :])
        for h in range(2):
            nc.sync.dma_start(out=x1[h][:], in_=rows(xf, 1)[:, 2 * h : 2 * h + 2, :])
        nc.sync.dma_start(out=ko1[:], in_=rows(ko, 1)[:, 0 : PACK - 1, :])
        for t in range(PACK - 1):
            nc.sync.dma_start(out=k1[t][:], in_=rows(kf, 1)[:, t, :])
        nc.sync.dma_start(out=ko_last[:], in_=rows(ko, 1)[:, PACK - 1, :])
        nc.sync.dma_start(out=k1[PACK - 1][:], in_=rows(kf, 1)[:, PACK - 1, :])
        nc.sync.dma_start(list_a[:], offs3)
        nc.sync.dma_start(out=rs_t[:], in_=rs.rearrange("(m p) c -> p m c", p=P))

        ident = keep.tile([P, P], F32, name="ident")
        make_identity(nc, ident[:])
        dealt = keep.tile([P, PACK, P], F32, name="dealt")
        nc.scalar.activation(dealt[:], ident[:].unsqueeze(1).to_broadcast([P, PACK, P]), COPY, scale=0.0)
        nc.vector.tensor_copy(
            dealt[: 2 * PASSES, :, :], vectors[: 2 * PASSES, :].rearrange("r (p t) -> r t p", t=PACK)
        )
        nc.scalar.activation(
            dealt[BIAS_ROW : BIAS_ROW + 1, :, : I // PACK],
            vectors[BIAS_ROW : BIAS_ROW + 1, :I].rearrange("r (p t) -> r t p", t=PACK),
            COPY,
        )
        turned = psum.tile([P, PACK, P], F32, name="turned")
        for t in range(PACK):
            nc.tensor.transpose(turned[:, t, :], dealt[:, t, :], ident[:])
        factors = keep.tile([P, PACK, 2 * PASSES], F32, name="factors")
        nc.vector.tensor_copy(factors[:], turned[:, :, : 2 * PASSES])
        bias_cols = keep.tile([P, PACK], F32, name="bias_cols")
        nc.vector.tensor_copy(bias_cols[:], turned[:, :, BIAS_ROW])
        bias_ps = psum.tile([P, PACK, P], F32, name="bias_ps")
        for t in range(PACK):
            nc.tensor.transpose(bias_ps[:, t, :], bias_cols[:, t : t + 1].to_broadcast([P, P]), ident[:])
        bias = keep.tile([P, I], F32, name="bias")
        nc.scalar.activation(
            bias[:].rearrange("p (n t) -> p n t", t=PACK),
            bias_ps[:, :, : I // PACK].rearrange("p t n -> p n t"),
            COPY,
        )

        xg = keep.tile([P, PASSES * PACK, PAD + J], F32, name="xg", tag="vectors_then_xg")
        nc.vector.memset(xg[:, :, PAD - 1 : PAD], 0.0)

        u_codes = [keep.tile([P, J], U32, name="u_codes%d" % a, align_bytes=64) for a in range(PASSES)]
        u_scales = [keep.tile([P, J], U8, name="u_scales%d" % a, align_bytes=64) for a in range(PASSES)]

        def quantise(codes, scales, woven):
            nc.vector.quantize_mx(
                out=codes.bitcast(E5M2X4), scales=scales, in_=woven[:].rearrange("p c t -> p (c t)")
            )

        def token_pass(a, windows):
            woven = keep.tile([P, J, PACK], BF16, name="u_woven%d" % a, align_bytes=64)
            diffs = []
            for t in range(PACK + 1):
                if t < PACK:
                    s = a * PACK + t
                    nc.scalar.activation(xg[:, s, PAD:], windows[t].indirect(list_x[:]), COPY)
                    diff = keep.tile([P, J], F32, name="diff%d" % s)
                    nc.vector.scalar_tensor_tensor(
                        diff[:], xg[:, s, PAD - 1 : PAD - 1 + J], -0.6, xg[:, s, PAD:], MULT, ADD
                    )
                    diffs.append(diff)
                if t > 0:
                    nc.vector.tensor_scalar(
                        woven[:, :, t - 1], diffs[t - 1][:], factors[:, t - 1, a : a + 1], None, MULT
                    )
            quantise(u_codes[a][:], u_scales[a][:], woven)

        acc = [[psum.tile([P, HALF], F32, name="acc%d_%d" % (m, h)) for h in range(2)] for m in range(2)]
        halves = [slice(0, HALF), slice(HALF, I)]

        def product(m, a, h, codes, scales):
            js = slice(m * P, (m + 1) * P)
            nc.tensor.matmul_mx(
                out=acc[m][h][:],
                lhsT=u_codes[a][:, js].bitcast(E5M2X4),
                lhsT_scale=u_scales[a][:, js],
                rhs=codes.bitcast(E5M2X4),
                rhs_scale=scales,
                start=(a == 0),
                stop=(a == PASSES - 1),
            )

        token_pass(0, [x0[:, t, :] for t in range(PACK)])
        woven0 = keep.tile([P, I, PACK], BF16, name="v_woven0", align_bytes=64)
        sums = []
        for t in range(PACK + 1):
            if t < PACK:
                kg = keep.tile([P, I], F32, name="kg0_%d" % t)
                nc.scalar.activation(kg[:], k0[t // 2][:, t % 2, :].indirect(list_k[:]), COPY)
                ks = keep.tile([P, I], F32, name="ks0_%d" % t)
                nc.vector.tensor_tensor(ks[:], kg[:], ko0[:, t, :], ADD)
                sums.append(ks)
            if t > 0:
                nc.vector.tensor_scalar(woven0[:, :, t - 1], sums[t - 1][:], factors[:, t - 1, PASSES : PASSES + 1], None, MULT)
        v_codes0 = keep.tile([P, I], U32, name="v_codes0", align_bytes=64)
        v_scales0 = keep.tile([P, I], U8, name="v_scales0", align_bytes=64)
        quantise(v_codes0[:], v_scales0[:], woven0)
        for m in range(2):
            for h in range(2):
                product(m, 0, h, v_codes0[:, halves[h]], v_scales0[:, halves[h]])

        token_pass(1, [x1[t // 2][:, t % 2, :] for t in range(PACK)])
        woven1 = [keep.tile([P, HALF, PACK], BF16, name="v_woven1_%d" % h, align_bytes=64) for h in range(2)]
        for t in range(PACK):
            own = ko1[:, t, :] if t < PACK - 1 else ko_last[:]
            ks = []
            for h in range(2):
                listed = k1[t][:].indirect(list_k[:, h * HALF // 16 : (h + 1) * HALF // 16])
                total = keep.tile([P, HALF], F32, name="ks1_%d_%d" % (t, h), tag="ks1_%d_%d" % (min(t, 2) if h == 0 else t, h))
                if t == PACK - 1 and h == 0:
                    nc.vector.tensor_tensor(total[:], listed, own[:, halves[h]], ADD)
                else:
                    kg = keep.tile([P, HALF], F32, name="kg1_%d_%d" % (t, h))
                    nc.scalar.activation(kg[:], listed, COPY)
                    nc.vector.tensor_tensor(total[:], kg[:], own[:, halves[h]], ADD)
                ks.append(total[:])
            for h in range(2):
                nc.vector.tensor_scalar(woven1[h][:, :, t], ks[h], factors[:, t, PASSES + 1 : PASSES + 2], None, MULT)
        for h in range(2):
            codes = keep.tile([P, HALF], U32, name="v_codes1_%d" % h, align_bytes=64)
            scales = keep.tile([P, HALF], U8, name="v_scales1_%d" % h, align_bytes=64)
            quantise(codes[:], scales[:], woven1[h])
            for m in range(2):
                product(m, 1, h, codes[:], scales[:])

        half_rs = keep.tile([P, 2, M], F32, name="half_rs")
        nc.scalar.activation(half_rs[:], rs_t[:], COPY, scale=0.5)

        scores = [keep.tile([P, I + PAD], F32, name="scores%d" % m) for m in range(2)]
        means = [keep.tile([P, 1], F32, name="mean%d" % m) for m in range(2)]
        for h in range(2):
            for m in range(2):
                nc.vector.tensor_tensor(scores[m][:, halves[h]], acc[m][h][:], bias[:, halves[h]], ADD)
            for m in range(2):
                mag = keep.tile([P, HALF + 1], F32, name="mag%d_%d" % (m, h))
                if h == 0:
                    nc.scalar.activation(mag[:, :HALF], scores[m][:, :HALF], ABS, accum_out=scores[m][:, I : I + 1])
                else:
                    nc.scalar.activation(
                        mag[:], scores[m][:, HALF : I + 1], ABS, scale=1.0 / I, accum_out=means[m][:]
                    )
        picked = [keep.tile([P, M], F32, name="picked%d" % m) for m in range(2)]
        nc.vector.tensor_copy(picked[0][:], scores[0][:, :I].indirect(list_a[:]))
        nc.scalar.activation(picked[1][:], scores[1][:, :I].indirect(list_a[:]), COPY)
        invs = [keep.tile([P, 1], F32, name="inv%d" % m) for m in range(2)]
        for m in range(2):
            nc.vector.reciprocal(invs[m][:], means[m][:])
        for m in range(2):
            y = keep.tile([P, M], F32, name="y%d" % m)
            nc.vector.scalar_tensor_tensor(y[:], picked[m][:], invs[m][:], half_rs[:, m, :], MULT, ADD)
            nc.sync.dma_start(out=out[m * P : (m + 1) * P, :], in_=y[:])
